import numpy as np
import ml_dtypes


def mxq(x, axis, fmt="e4m3"):
    dtype, down = {"e4m3": (ml_dtypes.float8_e4m3fn, 7), "e5m2": (ml_dtypes.float8_e5m2, 14)}[fmt]
    v = np.moveaxis(np.asarray(x, np.float32).astype(ml_dtypes.bfloat16).astype(np.float64), axis, -1)
    blocks = v.reshape(v.shape[:-1] + (-1, 32))
    amax = np.abs(blocks).max(-1, keepdims=True)
    byte = np.maximum(np.where(amax > 0, np.frexp(amax)[1] - 1 + 127, 0) - down, 1)
    scale = np.exp2(byte - 127.0)
    codes = (blocks / scale).astype(np.float32).astype(dtype).astype(np.float64)
    return np.moveaxis((codes * scale).reshape(v.shape), -1, axis)


WIDE = False


def mx_kscale(k):
    if not WIDE:
        return np.ones(k)
    levels = np.array([10, -10, 5, -5, 0])
    if k % 512:
        return np.exp2(np.random.permutation(np.resize(levels, k // 32))).repeat(32)
    a = np.empty((k // 512, 16))
    for p in range(k // 512):
        a[p, :8] = np.random.permutation(np.resize(levels, 8))
        for g in range(8):
            far = levels[np.abs(levels - a[p, g]) >= 10]
            a[p, g + 8] = far[np.random.randint(len(far))]
    return np.exp2(a.ravel()).repeat(32)


def f64(x):
    return np.asarray(x).astype(np.float64)


def striped(idx):
    return np.tile(idx.reshape(-1, 16).T, (8, 1)).astype(np.uint16)


def unstriped(offs):
    return offs[:16].T.reshape(-1).astype(np.int64)


def striped8(idx):
    return np.concatenate([x.reshape(-1, 16).T for x in idx]).astype(np.uint16)


def runs(offs, k):
    lists = np.stack([offs[16 * r : 16 * r + 16].T.reshape(-1) for r in range(8)]).astype(np.int64)
    return lists[np.arange(k) % 512 // 64]


def pack_weight(w):
    k, n = w.shape
    w = f64(np.asarray(w, np.float32).astype(ml_dtypes.bfloat16)).reshape(k // 32, 32, n)
    amax = np.abs(w).max(1)
    byte = np.clip(np.where(amax > 0, np.frexp(amax)[1] - 1 + 127 - 7, 1), 1, 254)
    scaled = (w * np.exp2(127.0 - byte)[:, None, :]).reshape(k, n).astype(np.float32)
    words = np.ascontiguousarray(scaled.reshape(k // 512, 128, 4, n).transpose(0, 1, 3, 2)).astype(ml_dtypes.float8_e4m3fn).view(np.uint8)
    return words, np.ascontiguousarray(byte.astype(np.uint8).reshape(k // 512, 16, n))


def unpack_weight(words, scales):
    g, p, n, _ = words.shape
    vals = np.ascontiguousarray(words).view(ml_dtypes.float8_e4m3fn).astype(np.float64) * np.repeat(np.exp2(scales.astype(np.float64) - 127.0), 8, axis=1)[..., None]
    return vals.transpose(0, 1, 3, 2).reshape(g * 512, n)


K, T, S, N, H = 512, 2048, 512, 512, 512


def setup_inputs():
    n = np.random.standard_normal
    s = mx_kscale(K)[:, None]
    u = mx_kscale(S)
    packed_xT = pack_weight(n((K, T)) * s)
    return {
        "x_words": packed_xT[0],
        "x_scales": packed_xT[1],
        "wa": (n((K, H)) / np.sqrt(K) / s).astype(np.float32),
        "wb": (n((K, N)) / np.sqrt(K) / s).astype(np.float32),
        "gt": (np.random.uniform(0.5, 1.5, (S, 1)) * u[:, None]).astype(np.float32),
        "gi": (np.random.uniform(0.5, 1.5, (S, 1)) / u[:, None]).astype(np.float32),
        "offs": striped(np.random.permutation(T)[:S]),
        "two": striped(np.random.permutation(T)[:S]),
        "fa": striped8(np.stack([np.random.permutation(H) for _ in range(8)])),
        "nb": striped8(np.stack([np.random.permutation(N) for _ in range(8)])),
    }


def reference(x_words, x_scales, wa, wb, gt, gi, offs, two, fa, nb):
    xq = unpack_weight(x_words, x_scales)[:, unstriped(offs)]
    a = xq.T @ mxq(f64(wa), 0, "e4m3")
    z = f64(gt) * (np.maximum(a, a[np.arange(S)[:, None], runs(fa, S)]))
    x_two = unpack_weight(x_words, x_scales)[:, unstriped(two)]
    b = x_two.T @ mxq(f64(wb), 0, "e4m3")
    z2 = f64(gi) * b
    cv = 0.0625 * ((mxq(z, 0, "e4m3").T @ mxq(z2, 0, "e4m3")))
    return np.maximum(cv, cv[np.arange(H)[:, None], runs(nb, H)])

@@ -1,0 +1,225 @@
+from contextlib import ExitStack
+
+import concourse.mybir as mybir
+from concourse.masks import make_identity
+
+K, T, S, N, H = 512, 2048, 512, 512, 512
+FLOPS = 2 * K * S * H + 2 * K * S * N + 2 * S * H * N
+
+F32 = mybir.dt.float32
+BF16 = mybir.dt.bfloat16
+I32 = mybir.dt.int32
+U32 = mybir.dt.uint32
+U16 = mybir.dt.uint16
+U8 = mybir.dt.uint8
+FP8X4 = mybir.dt.float8_e4m3fn_x4
+ACT = mybir.ActivationFunctionType
+ALU = mybir.AluOpType
+
+P = 128
+PACK = 4
+HALF = 256
+LIST_COLS = HALF // 16
+
+
+def tile_picked_mommax_none_p_kernel(
+    tc, x_words, x_scales, wa, wb, gt, gi, offs, two, fa, nb, out
+):
+    nc = tc.nc
+    with ExitStack() as ctx:
+        keep = ctx.enter_context(tc.tile_pool(name="keep", bufs=1))
+        psum = ctx.enter_context(tc.psum_pool(name="psum", bufs=1))
+
+        def sb(name, shape, dtype):
+            return keep.tile(shape, dtype, name=name, align_bytes=64)
+
+        def bank(tag, name):
+            return psum.tile([P, 512], F32, name=name, tag=tag)
+
+        offs_l = sb("offs_l", [P, S // 16], U16)
+        two_l = sb("two_l", [P, S // 16], U16)
+        fa_l = sb("fa_l", [P, H // 16], U16)
+        nb_l = sb("nb_l", [P, N // 16], U16)
+        xs = sb("xs", [P, T], U8)
+        xw = sb("xw", [P, T], I32)
+
+        def raw(name, h):
+            return keep.tile([P, PACK, HALF], F32, name=name, tag="raw%d" % h, align_bytes=64)
+
+        wa_raw = [raw("wa_raw%d" % h, h) for h in range(2)]
+        rows = sb("rows", [P, P], F32)
+        ident = sb("ident", [P, P], F32)
+
+        nc.gpsimd.memset(xs[:].bitcast(I32), 0)
+        nc.gpsimd.memset(rows[:], 0.0)
+        make_identity(nc, ident[:])
+
+        nc.sync.dma_start(offs_l[:], offs)
+        nc.sync.dma_start(two_l[:], two)
+        for q in range(4):
+            nc.sync.dma_start(xs[32 * q : 32 * q + 4, :].bitcast(I32), x_scales[0, 4 * q : 4 * q + 4, :].bitcast(I32))
+        wa_v = wa.rearrange("(p j) c -> p j c", j=PACK)
+        for h in range(2):
+            nc.sync.dma_start(wa_raw[h][:], wa_v[:, :, HALF * h : HALF * (h + 1)])
+        nc.sync.dma_start(xw[:], x_words[0].rearrange("p c r -> p (c r)").bitcast(I32))
+        for r, g in enumerate((gt, gi)):
+            nc.scalar.dma_start(
+                rows[PACK * r : PACK * (r + 1), :].rearrange("t (q e) -> t q e", e=8),
+                g.rearrange("(q t e) o -> t q (e o)", t=PACK, e=8),
+            )
+        nc.sync.dma_start(fa_l[:], fa)
+        nc.sync.dma_start(nb_l[:], nb)
+
+        def gather_scales(name, lst):
+            picked = sb(name + "_picked", [P, S], U8)
+            dealt = sb(name + "_dealt", [P, S], U8)
+            nc.vector.tensor_copy(picked[:], xs[:].indirect(lst[:]))
+            nc.vector.tensor_copy(
+                dealt[:].bitcast(I32).rearrange("p (t q w) -> p t q w", t=PACK, w=2),
+                picked[:].bitcast(I32).rearrange("p (q t w) -> p t q w", t=PACK, w=2),
+            )
+            return dealt
+
+        def gather_words(name, lst):
+            dealt = sb(name, [P, S], U32)
+            nc.vector.tensor_copy(
+                dealt[:].rearrange("p (t q e) -> p q t e", t=PACK, e=8), xw[:].bitcast(U32).indirect(lst[:])
+            )
+            return dealt
+
+        def weave(dst):
+            return dst.rearrange("p (c i) t -> p c t i", i=4)
+
+        def planes(src):
+            return src.rearrange("p t (c i) -> p c t i", i=4)
+
+        def quantize(codes, scales, woven):
+            nc.vector.quantize_mx(out=codes.bitcast(FP8X4), scales=scales, in_=woven.rearrange("p c t -> p (c t)"))
+
+        def mx(acc, lhs, lhs_s, rhs, rhs_s):
+            nc.tensor.matmul_mx(
+                out=acc[:], lhsT=lhs.bitcast(FP8X4), lhsT_scale=lhs_s, rhs=rhs.bitcast(FP8X4), rhs_scale=rhs_s,
+                start=True, stop=True,
+            )
+
+        xa_s = gather_scales("xa_s", offs_l)
+        xb_s = gather_scales("xb_s", two_l)
+
+        wa_q = sb("wa_q", [P, H], U32)
+        wa_s = sb("wa_s", [P, H], U8)
+        for h in range(2):
+            cols = slice(HALF * h, HALF * (h + 1))
+            woven = sb("wa_bf%d" % h, [P, HALF, PACK], BF16)
+            nc.scalar.copy(weave(woven[:]), planes(wa_raw[h][:]))
+            quantize(wa_q[:, cols], wa_s[:, cols], woven[:])
+
+        wb_raw = [raw("wb_raw%d" % h, h) for h in range(2)]
+        wb_v = wb.rearrange("(p j) c -> p j c", j=PACK)
+        for h in range(2):
+            nc.sync.dma_start(wb_raw[h][:], wb_v[:, :, HALF * h : HALF * (h + 1)])
+
+        turned = bank("b3", "turned")
+        nc.tensor.transpose(turned[:, :P], rows[:], ident[:])
+        gt_abs = sb("gt_abs", [P, PACK], F32)
+        gt_sign = sb("gt_sign", [P, PACK], F32)
+        gi_signed = sb("gi_signed", [P, PACK], F32)
+        nc.scalar.activation(gt_abs[:], turned[:, 0:PACK], ACT.Abs)
+        nc.scalar.activation(gt_sign[:], turned[:, 0:PACK], ACT.Sign)
+        for t in range(PACK):
+            nc.scalar.activation(
+                gi_signed[:, t : t + 1], turned[:, PACK + t : PACK + t + 1], ACT.Copy, scale=gt_sign[:, t : t + 1]
+            )
+
+        xa_w = gather_words("xa_w", offs_l)
+        xb_w = gather_words("xb_w", two_l)
+
+        a_all = sb("a_all", [P, PACK, H], F32)
+        a_fetched = sb("a_fetched", [P, PACK, H], F32)
+        for t in range(PACK):
+            m = slice(P * t, P * (t + 1))
+            acc = bank("a%d" % t, "acc_a%d" % t)
+            mx(acc, xa_w[:, m], xa_s[:, m], wa_q[:], wa_s[:])
+            win = sb("a_win%d" % t, [P, H], F32)
+            nc.scalar.activation(win[:], acc[:], ACT.Copy, scale=gt_abs[:, t : t + 1])
+            nc.sync.dma_start(a_all[:, t, :], win[:])
+            for h in range(2):
+                nc.vector.tensor_copy(
+                    a_fetched[:, t, HALF * h : HALF * (h + 1)],
+                    win[:].indirect(fa_l[:, LIST_COLS * h : LIST_COLS * (h + 1)]),
+                )
+
+        wb_q = sb("wb_q", [P, N], U32)
+        wb_s = sb("wb_s", [P, N], U8)
+        for h in range(2):
+            cols = slice(HALF * h, HALF * (h + 1))
+            woven = sb("wb_bf%d" % h, [P, HALF, PACK], BF16)
+            nc.scalar.copy(weave(woven[:]), planes(wb_raw[h][:]))
+            quantize(wb_q[:, cols], wb_s[:, cols], woven[:])
+
+        z2_planes = sb("z2_planes", [P, PACK, N], BF16)
+        for t in range(PACK):
+            m = slice(P * t, P * (t + 1))
+            acc = bank("b%d" % t, "acc_b%d" % t)
+            mx(acc, xb_w[:, m], xb_s[:, m], wb_q[:], wb_s[:])
+            nc.scalar.activation(z2_planes[:, t, :], acc[:], ACT.Copy, scale=gi_signed[:, t : t + 1])
+
+        z_bf = [sb("z_bf%d" % u, [P, P, PACK], BF16) for u in range(PACK)]
+        z_q = [sb("z_q%d" % u, [P, P], U32) for u in range(PACK)]
+        z_s = [sb("z_s%d" % u, [P, P], U8) for u in range(PACK)]
+
+        def pool_z(u):
+            def pick(src):
+                return src[:].rearrange("p t (v u i) -> p u v t i", u=PACK, i=4)[:, u]
+
+            nc.vector.tensor_tensor(weave(z_bf[u][:]), pick(a_all), pick(a_fetched), ALU.max)
+
+        def quantize_z(u):
+            quantize(z_q[u][:], z_s[u][:], z_bf[u][:])
+
+        z2_q = sb("z2_q", [P, N], U32)
+        z2_s = sb("z2_s", [P, N], U8)
+        z2_bf = [sb("z2_bf%d" % h, [P, HALF, PACK], BF16) for h in range(2)]
+
+        pool_z(0)
+        pool_z(1)
+        quantize_z(0)
+        nc.scalar.copy(weave(z2_bf[0][:]), planes(z2_planes[:, :, 0:HALF]))
+        nc.vector.tensor_copy(weave(z2_bf[1][:]), planes(z2_planes[:, :, HALF:N]))
+        quantize_z(1)
+        for h in (1, 0):
+            cols = slice(HALF * h, HALF * (h + 1))
+            quantize(z2_q[:, cols], z2_s[:, cols], z2_bf[h][:])
+        pool_z(2)
+        pool_z(3)
+        quantize_z(2)
+        quantize_z(3)
+
+        out_v = out.rearrange("(v u i) n -> u v i n", u=PACK, i=4)
+        wins, fetched = [], []
+
+        def fetch(u):
+            acc = bank("a%d" % u, "acc_cv%d" % u)
+            mx(acc, z_q[u][:], z_s[u][:], z2_q[:], z2_s[:])
+            win = sb("cv_win%d" % u, [P, N], F32)
+            nc.scalar.activation(win[:], acc[:], ACT.Copy, scale=0.0625)
+            got = sb("cv_fetched%d" % u, [P, N], F32)
+            for h in range(2):
+                nc.vector.tensor_copy(
+                    got[:, HALF * h : HALF * (h + 1)], win[:].indirect(nb_l[:, LIST_COLS * h : LIST_COLS * (h + 1)])
+                )
+            wins.append(win)
+            fetched.append(got)
+
+        def finish(u, pieces):
+            width = N // pieces
+            for c in range(pieces):
+                cols = slice(width * c, width * (c + 1))
+                res = sb("res%d_%d" % (u, c), [P, width], F32)
+                nc.vector.tensor_tensor(res[:], wins[u][:, cols], fetched[u][:, cols], ALU.max)
+                nc.sync.dma_start(out_v[u][:, :, cols], res[:])
+
+        fetch(0)
+        for u in range(1, PACK):
+            fetch(u)
+            finish(u - 1, 1)
+        finish(PACK - 1, 2)

@@ -19,6 +19,7 @@ ALU = mybir.AluOpType
 P = 128
 PACK = 4
 HALF = 256
+EARLY = 384
 LIST_COLS = HALF // 16
 
 
@@ -30,8 +31,8 @@ def tile_picked_mommax_none_p_kernel(
         keep = ctx.enter_context(tc.tile_pool(name="keep", bufs=1))
         psum = ctx.enter_context(tc.psum_pool(name="psum", bufs=1))
 
-        def sb(name, shape, dtype):
-            return keep.tile(shape, dtype, name=name, align_bytes=64)
+        def sb(name, shape, dtype, tag=None):
+            return keep.tile(shape, dtype, name=name, tag=tag or name, align_bytes=64)
 
         def bank(tag, name):
             return psum.tile([P, 512], F32, name=name, tag=tag)
@@ -42,32 +43,32 @@ def tile_picked_mommax_none_p_kernel(
         nb_l = sb("nb_l", [P, N // 16], U16)
         xs = sb("xs", [P, T], U8)
         xw = sb("xw", [P, T], I32)
-
-        def raw(name, h):
-            return keep.tile([P, PACK, HALF], F32, name=name, tag="raw%d" % h, align_bytes=64)
-
-        wa_raw = [raw("wa_raw%d" % h, h) for h in range(2)]
+        wa_raw = [sb("wa_raw0", [P, PACK, EARLY], F32), sb("wa_raw1", [P, PACK, H - EARLY], F32)]
+        wb_raw = [sb("wb_raw%d" % h, [P, PACK, HALF], F32) for h in range(2)]
         rows = sb("rows", [P, P], F32)
         ident = sb("ident", [P, P], F32)
 
         nc.gpsimd.memset(xs[:].bitcast(I32), 0)
         nc.gpsimd.memset(rows[:], 0.0)
-        make_identity(nc, ident[:])
 
         nc.sync.dma_start(offs_l[:], offs)
         nc.sync.dma_start(two_l[:], two)
         for q in range(4):
             nc.sync.dma_start(xs[32 * q : 32 * q + 4, :].bitcast(I32), x_scales[0, 4 * q : 4 * q + 4, :].bitcast(I32))
         wa_v = wa.rearrange("(p j) c -> p j c", j=PACK)
-        for h in range(2):
-            nc.sync.dma_start(wa_raw[h][:], wa_v[:, :, HALF * h : HALF * (h + 1)])
+        nc.sync.dma_start(wa_raw[0][:], wa_v[:, :, 0:EARLY])
         nc.sync.dma_start(xw[:], x_words[0].rearrange("p c r -> p (c r)").bitcast(I32))
         for r, g in enumerate((gt, gi)):
-            nc.scalar.dma_start(
+            nc.sync.dma_start(
                 rows[PACK * r : PACK * (r + 1), :].rearrange("t (q e) -> t q e", e=8),
                 g.rearrange("(q t e) o -> t q (e o)", t=PACK, e=8),
             )
+        make_identity(nc, ident[:])
+        nc.sync.dma_start(wa_raw[1][:], wa_v[:, :, EARLY:H])
         nc.sync.dma_start(fa_l[:], fa)
+        wb_v = wb.rearrange("(p j) c -> p j c", j=PACK)
+        for h in range(2):
+            nc.sync.dma_start(wb_raw[h][:], wb_v[:, :, HALF * h : HALF * (h + 1)])
         nc.sync.dma_start(nb_l[:], nb)
 
         def gather_scales(name, lst):
@@ -80,8 +81,8 @@ def tile_picked_mommax_none_p_kernel(
             )
             return dealt
 
-        def gather_words(name, lst):
-            dealt = sb(name, [P, S], U32)
+        def gather_words(name, lst, tag):
+            dealt = sb(name, [P, S], U32, tag)
             nc.vector.tensor_copy(
                 dealt[:].rearrange("p (t q e) -> p q t e", t=PACK, e=8), xw[:].bitcast(U32).indirect(lst[:])
             )
@@ -107,16 +108,16 @@ def tile_picked_mommax_none_p_kernel(
 
         wa_q = sb("wa_q", [P, H], U32)
         wa_s = sb("wa_s", [P, H], U8)
-        for h in range(2):
-            cols = slice(HALF * h, HALF * (h + 1))
-            woven = sb("wa_bf%d" % h, [P, HALF, PACK], BF16)
-            nc.scalar.copy(weave(woven[:]), planes(wa_raw[h][:]))
-            quantize(wa_q[:, cols], wa_s[:, cols], woven[:])
+        woven = sb("wa_bf0", [P, EARLY, PACK], BF16)
+        nc.scalar.copy(weave(woven[:]), planes(wa_raw[0][:]))
+        for cols in (slice(0, HALF), slice(HALF, EARLY)):
+            quantize(wa_q[:, cols], wa_s[:, cols], woven[:, cols, :])
 
-        wb_raw = [raw("wb_raw%d" % h, h) for h in range(2)]
-        wb_v = wb.rearrange("(p j) c -> p j c", j=PACK)
-        for h in range(2):
-            nc.sync.dma_start(wb_raw[h][:], wb_v[:, :, HALF * h : HALF * (h + 1)])
+        xa_w = gather_words("xa_w", offs_l, None)
+        woven = sb("wa_bf1", [P, H - EARLY, PACK], BF16)
+        nc.scalar.copy(weave(woven[:]), planes(wa_raw[1][:]))
+        quantize(wa_q[:, EARLY:H], wa_s[:, EARLY:H], woven[:])
+        xb_w = gather_words("xb_w", two_l, "wa_bf1")
 
         turned = bank("b3", "turned")
         nc.tensor.transpose(turned[:, :P], rows[:], ident[:])
@@ -125,17 +126,15 @@ def tile_picked_mommax_none_p_kernel(
         gi_signed = sb("gi_signed", [P, PACK], F32)
         nc.scalar.activation(gt_abs[:], turned[:, 0:PACK], ACT.Abs)
         nc.scalar.activation(gt_sign[:], turned[:, 0:PACK], ACT.Sign)
-        for t in range(PACK):
-            nc.scalar.activation(
-                gi_signed[:, t : t + 1], turned[:, PACK + t : PACK + t + 1], ACT.Copy, scale=gt_sign[:, t : t + 1]
-            )
-
-        xa_w = gather_words("xa_w", offs_l)
-        xb_w = gather_words("xb_w", two_l)
+        nc.vector.tensor_tensor(gi_signed[:], turned[:, PACK : 2 * PACK], gt_sign[:], ALU.mult)
 
         a_all = sb("a_all", [P, PACK, H], F32)
         a_fetched = sb("a_fetched", [P, PACK, H], F32)
-        for t in range(PACK):
+        wb_q = sb("wb_q", [P, N], U32)
+        wb_s = sb("wb_s", [P, N], U8)
+        wb_bf = [sb("wb_bf%d" % h, [P, HALF, PACK], BF16) for h in range(2)]
+
+        def project_a(t):
             m = slice(P * t, P * (t + 1))
             acc = bank("a%d" % t, "acc_a%d" % t)
             mx(acc, xa_w[:, m], xa_s[:, m], wa_q[:], wa_s[:])
@@ -148,13 +147,21 @@ def tile_picked_mommax_none_p_kernel(
                     win[:].indirect(fa_l[:, LIST_COLS * h : LIST_COLS * (h + 1)]),
                 )
 
-        wb_q = sb("wb_q", [P, N], U32)
-        wb_s = sb("wb_s", [P, N], U8)
-        for h in range(2):
-            cols = slice(HALF * h, HALF * (h + 1))
-            woven = sb("wb_bf%d" % h, [P, HALF, PACK], BF16)
-            nc.scalar.copy(weave(woven[:]), planes(wb_raw[h][:]))
-            quantize(wb_q[:, cols], wb_s[:, cols], woven[:])
+        def round_wb(quarter):
+            h, c = divmod(quarter, 2)
+            cols = slice(P * c, P * (c + 1))
+            nc.scalar.copy(weave(wb_bf[h][:, cols, :]), planes(wb_raw[h][:, :, cols]))
+            if c == 1:
+                cols = slice(HALF * h, HALF * (h + 1))
+                quantize(wb_q[:, cols], wb_s[:, cols], wb_bf[h][:])
+
+        project_a(0)
+        round_wb(0)
+        project_a(1)
+        for quarter in (1, 2, 3):
+            round_wb(quarter)
+        project_a(2)
+        project_a(3)
 
         z2_planes = sb("z2_planes", [P, PACK, N], BF16)
         for t in range(PACK):
@@ -163,63 +170,40 @@ def tile_picked_mommax_none_p_kernel(
             mx(acc, xb_w[:, m], xb_s[:, m], wb_q[:], wb_s[:])
             nc.scalar.activation(z2_planes[:, t, :], acc[:], ACT.Copy, scale=gi_signed[:, t : t + 1])
 
-        z_bf = [sb("z_bf%d" % u, [P, P, PACK], BF16) for u in range(PACK)]
-        z_q = [sb("z_q%d" % u, [P, P], U32) for u in range(PACK)]
-        z_s = [sb("z_s%d" % u, [P, P], U8) for u in range(PACK)]
+        z_q = [sb("z_q%d" % h, [P, 2 * P], U32) for h in range(2)]
+        z_s = [sb("z_s%d" % h, [P, 2 * P], U8) for h in range(2)]
 
-        def pool_z(u):
-            def pick(src):
-                return src[:].rearrange("p t (v u i) -> p u v t i", u=PACK, i=4)[:, u]
-
-            nc.vector.tensor_tensor(weave(z_bf[u][:]), pick(a_all), pick(a_fetched), ALU.max)
-
-        def quantize_z(u):
-            quantize(z_q[u][:], z_s[u][:], z_bf[u][:])
+        def pool_z(h, tag):
+            woven = sb("z_bf%d" % h, [P, 2 * P, PACK], BF16, tag)
+            for c in range(2):
+                a_part, fetched_part = (
+                    src[:].rearrange("p t (v u i) -> p u v t i", u=PACK, i=4)[:, 2 * h + c] for src in (a_all, a_fetched)
+                )
+                nc.vector.tensor_tensor(weave(woven[:, P * c : P * (c + 1), :]), a_part, fetched_part, ALU.max)
+            quantize(z_q[h][:], z_s[h][:], woven[:])
 
         z2_q = sb("z2_q", [P, N], U32)
         z2_s = sb("z2_s", [P, N], U8)
-        z2_bf = [sb("z2_bf%d" % h, [P, HALF, PACK], BF16) for h in range(2)]
+        z2_bf = sb("z2_bf", [P, N, PACK], BF16)
 
-        pool_z(0)
-        pool_z(1)
-        quantize_z(0)
-        nc.scalar.copy(weave(z2_bf[0][:]), planes(z2_planes[:, :, 0:HALF]))
-        nc.vector.tensor_copy(weave(z2_bf[1][:]), planes(z2_planes[:, :, HALF:N]))
-        quantize_z(1)
-        for h in (1, 0):
-            cols = slice(HALF * h, HALF * (h + 1))
-            quantize(z2_q[:, cols], z2_s[:, cols], z2_bf[h][:])
-        pool_z(2)
-        pool_z(3)
-        quantize_z(2)
-        quantize_z(3)
+        pool_z(0, None)
+        nc.scalar.copy(weave(z2_bf[:, 0:HALF, :]), planes(z2_planes[:, :, 0:HALF]))
+        nc.vector.tensor_copy(weave(z2_bf[:, HALF:N, :]), planes(z2_planes[:, :, HALF:N]))
+        quantize(z2_q[:], z2_s[:], z2_bf[:])
+        pool_z(1, "z2_bf")
 
         out_v = out.rearrange("(v u i) n -> u v i n", u=PACK, i=4)
-        wins, fetched = [], []
-
-        def fetch(u):
+        for u in range(PACK):
             acc = bank("a%d" % u, "acc_cv%d" % u)
-            mx(acc, z_q[u][:], z_s[u][:], z2_q[:], z2_s[:])
+            m = slice(P * (u % 2), P * (u % 2 + 1))
+            mx(acc, z_q[u // 2][:, m], z_s[u // 2][:, m], z2_q[:], z2_s[:])
             win = sb("cv_win%d" % u, [P, N], F32)
             nc.scalar.activation(win[:], acc[:], ACT.Copy, scale=0.0625)
-            got = sb("cv_fetched%d" % u, [P, N], F32)
+            got = [sb("cv_fetched%d_%d" % (u, h), [P, HALF], F32) for h in range(2)]
             for h in range(2):
-                nc.vector.tensor_copy(
-                    got[:, HALF * h : HALF * (h + 1)], win[:].indirect(nb_l[:, LIST_COLS * h : LIST_COLS * (h + 1)])
-                )
-            wins.append(win)
-            fetched.append(got)
-
-        def finish(u, pieces):
-            width = N // pieces
-            for c in range(pieces):
-                cols = slice(width * c, width * (c + 1))
-                res = sb("res%d_%d" % (u, c), [P, width], F32)
-                nc.vector.tensor_tensor(res[:], wins[u][:, cols], fetched[u][:, cols], ALU.max)
+                nc.vector.tensor_copy(got[h][:], win[:].indirect(nb_l[:, LIST_COLS * h : LIST_COLS * (h + 1)]))
+            for h in range(2):
+                cols = slice(HALF * h, HALF * (h + 1))
+                res = sb("res%d_%d" % (u, h), [P, HALF], F32)
+                nc.vector.tensor_tensor(res[:], win[:, cols], got[h][:], ALU.max)
                 nc.sync.dma_start(out_v[u][:, :, cols], res[:])
-
-        fetch(0)
-        for u in range(1, PACK):
-            fetch(u)
-            finish(u - 1, 1)
-        finish(PACK - 1, 2)

@@ -20,6 +20,7 @@ P = 128
 PACK = 4
 HALF = 256
 EARLY = 384
+SHARE = 384
 LIST_COLS = HALF // 16
 
 
@@ -43,20 +44,24 @@ def tile_picked_mommax_none_p_kernel(
         nb_l = sb("nb_l", [P, N // 16], U16)
         xs = sb("xs", [P, T], U8)
         xw = sb("xw", [P, T], I32)
-        wa_raw = [sb("wa_raw0", [P, PACK, EARLY], F32), sb("wa_raw1", [P, PACK, H - EARLY], F32)]
-        wb_raw = [sb("wb_raw%d" % h, [P, PACK, HALF], F32) for h in range(2)]
+        wa_early = sb("wa_early", [P, PACK, EARLY], F32)
         rows = sb("rows", [P, P], F32)
         ident = sb("ident", [P, P], F32)
 
         nc.gpsimd.memset(xs[:].bitcast(I32), 0)
         nc.gpsimd.memset(rows[:], 0.0)
+        wins = [sb("win%d" % t, [P, 2 * H], F32) for t in range(PACK)]
+        for win in wins:
+            nc.vector.memset(win[:, H:], 0.0)
+        wa_late = sb("wa_late", [P, PACK, H - EARLY], F32)[:]
+        wb_raw = [sb("wb_raw%d" % h, [P, PACK, HALF], F32)[:] for h in range(2)]
 
         nc.sync.dma_start(offs_l[:], offs)
         nc.sync.dma_start(two_l[:], two)
         for q in range(4):
             nc.sync.dma_start(xs[32 * q : 32 * q + 4, :].bitcast(I32), x_scales[0, 4 * q : 4 * q + 4, :].bitcast(I32))
         wa_v = wa.rearrange("(p j) c -> p j c", j=PACK)
-        nc.sync.dma_start(wa_raw[0][:], wa_v[:, :, 0:EARLY])
+        nc.sync.dma_start(wa_early[:], wa_v[:, :, 0:EARLY])
         nc.sync.dma_start(xw[:], x_words[0].rearrange("p c r -> p (c r)").bitcast(I32))
         for r, g in enumerate((gt, gi)):
             nc.sync.dma_start(
@@ -64,11 +69,11 @@ def tile_picked_mommax_none_p_kernel(
                 g.rearrange("(q t e) o -> t q (e o)", t=PACK, e=8),
             )
         make_identity(nc, ident[:])
-        nc.sync.dma_start(wa_raw[1][:], wa_v[:, :, EARLY:H])
+        nc.sync.dma_start(wa_late, wa_v[:, :, EARLY:H])
         nc.sync.dma_start(fa_l[:], fa)
         wb_v = wb.rearrange("(p j) c -> p j c", j=PACK)
         for h in range(2):
-            nc.sync.dma_start(wb_raw[h][:], wb_v[:, :, HALF * h : HALF * (h + 1)])
+            nc.sync.dma_start(wb_raw[h], wb_v[:, :, HALF * h : HALF * (h + 1)])
         nc.sync.dma_start(nb_l[:], nb)
 
         def gather_scales(name, lst):
@@ -99,7 +104,7 @@ def tile_picked_mommax_none_p_kernel(
 
         def mx(acc, lhs, lhs_s, rhs, rhs_s):
             nc.tensor.matmul_mx(
-                out=acc[:], lhsT=lhs.bitcast(FP8X4), lhsT_scale=lhs_s, rhs=rhs.bitcast(FP8X4), rhs_scale=rhs_s,
+                out=acc, lhsT=lhs.bitcast(FP8X4), lhsT_scale=lhs_s, rhs=rhs.bitcast(FP8X4), rhs_scale=rhs_s,
                 start=True, stop=True,
             )
 
@@ -109,15 +114,17 @@ def tile_picked_mommax_none_p_kernel(
         wa_q = sb("wa_q", [P, H], U32)
         wa_s = sb("wa_s", [P, H], U8)
         woven = sb("wa_bf0", [P, EARLY, PACK], BF16)
-        nc.scalar.copy(weave(woven[:]), planes(wa_raw[0][:]))
+        nc.scalar.copy(weave(woven[:]), planes(wa_early[:]))
         for cols in (slice(0, HALF), slice(HALF, EARLY)):
             quantize(wa_q[:, cols], wa_s[:, cols], woven[:, cols, :])
 
         xa_w = gather_words("xa_w", offs_l, None)
-        woven = sb("wa_bf1", [P, H - EARLY, PACK], BF16)
-        nc.scalar.copy(weave(woven[:]), planes(wa_raw[1][:]))
-        quantize(wa_q[:, EARLY:H], wa_s[:, EARLY:H], woven[:])
-        xb_w = gather_words("xb_w", two_l, "wa_bf1")
+        a_fetched = sb("a_fetched", [P, PACK * H], F32)
+        wb_bf = a_fetched[:, 3 * HALF : 7 * HALF].bitcast(BF16).rearrange("p (c t) -> p c t", t=PACK)
+        woven = wb_bf[:, 0 : H - EARLY, :]
+        nc.scalar.copy(weave(woven), planes(wa_late))
+        quantize(wa_q[:, EARLY:H], wa_s[:, EARLY:H], woven)
+        xb_w = gather_words("xb_w", two_l, "wa_late")
 
         turned = bank("b3", "turned")
         nc.tensor.transpose(turned[:, :P], rows[:], ident[:])
@@ -128,46 +135,28 @@ def tile_picked_mommax_none_p_kernel(
         nc.scalar.activation(gt_sign[:], turned[:, 0:PACK], ACT.Sign)
         nc.vector.tensor_tensor(gi_signed[:], turned[:, PACK : 2 * PACK], gt_sign[:], ALU.mult)
 
-        a_all = sb("a_all", [P, PACK, H], F32)
-        a_fetched = sb("a_fetched", [P, PACK, H], F32)
         wb_q = sb("wb_q", [P, N], U32)
         wb_s = sb("wb_s", [P, N], U8)
-        wb_bf = [sb("wb_bf%d" % h, [P, HALF, PACK], BF16) for h in range(2)]
+        for h in range(2):
+            nc.gpsimd.tensor_scalar(
+                wb_bf[:, HALF * h : HALF * (h + 1), :], wb_raw[h].rearrange("p t c -> p c t"), 1.0, 0.0, ALU.mult, ALU.add
+            )
+        quantize(wb_q[:], wb_s[:], wb_bf)
 
-        def project_a(t):
+        a_all = sb("a_all", [P, PACK * H], F32)
+        for t in range(PACK):
             m = slice(P * t, P * (t + 1))
             acc = bank("a%d" % t, "acc_a%d" % t)
-            mx(acc, xa_w[:, m], xa_s[:, m], wa_q[:], wa_s[:])
-            win = sb("a_win%d" % t, [P, H], F32)
-            nc.scalar.activation(win[:], acc[:], ACT.Copy, scale=gt_abs[:, t : t + 1])
-            nc.sync.dma_start(a_all[:, t, :], win[:])
-            for h in range(2):
-                nc.vector.tensor_copy(
-                    a_fetched[:, t, HALF * h : HALF * (h + 1)],
-                    win[:].indirect(fa_l[:, LIST_COLS * h : LIST_COLS * (h + 1)]),
-                )
-
-        def round_wb(quarter):
-            h, c = divmod(quarter, 2)
-            cols = slice(P * c, P * (c + 1))
-            nc.scalar.copy(weave(wb_bf[h][:, cols, :]), planes(wb_raw[h][:, :, cols]))
-            if c == 1:
-                cols = slice(HALF * h, HALF * (h + 1))
-                quantize(wb_q[:, cols], wb_s[:, cols], wb_bf[h][:])
-
-        project_a(0)
-        round_wb(0)
-        project_a(1)
-        for quarter in (1, 2, 3):
-            round_wb(quarter)
-        project_a(2)
-        project_a(3)
+            mx(acc[:], xa_w[:, m], xa_s[:, m], wa_q[:], wa_s[:])
+            nc.scalar.activation(wins[t][:, :H], acc[:], ACT.Copy, scale=gt_abs[:, t : t + 1])
+            nc.sync.dma_start(a_all[:, H * t : H * (t + 1)], wins[t][:, :H])
+            nc.vector.tensor_copy(a_fetched[:, H * t : H * (t + 1)], wins[t][:].indirect(fa_l[:]))
 
         z2_planes = sb("z2_planes", [P, PACK, N], BF16)
         for t in range(PACK):
             m = slice(P * t, P * (t + 1))
             acc = bank("b%d" % t, "acc_b%d" % t)
-            mx(acc, xb_w[:, m], xb_s[:, m], wb_q[:], wb_s[:])
+            mx(acc[:], xb_w[:, m], xb_s[:, m], wb_q[:], wb_s[:])
             nc.scalar.activation(z2_planes[:, t, :], acc[:], ACT.Copy, scale=gi_signed[:, t : t + 1])
 
         z_q = [sb("z_q%d" % h, [P, 2 * P], U32) for h in range(2)]
@@ -177,9 +166,10 @@ def tile_picked_mommax_none_p_kernel(
             woven = sb("z_bf%d" % h, [P, 2 * P, PACK], BF16, tag)
             for c in range(2):
                 a_part, fetched_part = (
-                    src[:].rearrange("p t (v u i) -> p u v t i", u=PACK, i=4)[:, 2 * h + c] for src in (a_all, a_fetched)
+                    src[:].rearrange("p (t v u i) -> p u v t i", t=PACK, u=PACK, i=2)[:, 2 * h + c] for src in (a_all, a_fetched)
                 )
-                nc.vector.tensor_tensor(weave(woven[:, P * c : P * (c + 1), :]), a_part, fetched_part, ALU.max)
+                dst = woven[:, P * c : P * (c + 1), :].rearrange("p (v i) t -> p v t i", i=2)
+                nc.vector.tensor_tensor(dst, a_part, fetched_part, ALU.max)
             quantize(z_q[h][:], z_s[h][:], woven[:])
 
         z2_q = sb("z2_q", [P, N], U32)
@@ -187,23 +177,35 @@ def tile_picked_mommax_none_p_kernel(
         z2_bf = sb("z2_bf", [P, N, PACK], BF16)
 
         pool_z(0, None)
-        nc.scalar.copy(weave(z2_bf[:, 0:HALF, :]), planes(z2_planes[:, :, 0:HALF]))
-        nc.vector.tensor_copy(weave(z2_bf[:, HALF:N, :]), planes(z2_planes[:, :, HALF:N]))
+        nc.scalar.copy(weave(z2_bf[:, 0:SHARE, :]), planes(z2_planes[:, :, 0:SHARE]))
+        nc.vector.tensor_copy(weave(z2_bf[:, SHARE:N, :]), planes(z2_planes[:, :, SHARE:N]))
         quantize(z2_q[:], z2_s[:], z2_bf[:])
         pool_z(1, "z2_bf")
 
-        out_v = out.rearrange("(v u i) n -> u v i n", u=PACK, i=4)
-        for u in range(PACK):
+        out_v = out.rearrange("(v u i) n -> u v i n", u=PACK, i=2)
+        got = [sb("cv_fetched%d" % u, [P, N], F32, "z2_bf" if u == 1 else None) for u in range(PACK)]
+
+        def fetch(u, pieces):
             acc = bank("a%d" % u, "acc_cv%d" % u)
             m = slice(P * (u % 2), P * (u % 2 + 1))
-            mx(acc, z_q[u // 2][:, m], z_s[u // 2][:, m], z2_q[:], z2_s[:])
-            win = sb("cv_win%d" % u, [P, N], F32)
-            nc.scalar.activation(win[:], acc[:], ACT.Copy, scale=0.0625)
-            got = [sb("cv_fetched%d_%d" % (u, h), [P, HALF], F32) for h in range(2)]
-            for h in range(2):
-                nc.vector.tensor_copy(got[h][:], win[:].indirect(nb_l[:, LIST_COLS * h : LIST_COLS * (h + 1)]))
-            for h in range(2):
-                cols = slice(HALF * h, HALF * (h + 1))
-                res = sb("res%d_%d" % (u, h), [P, HALF], F32)
-                nc.vector.tensor_tensor(res[:], win[:, cols], got[h][:], ALU.max)
-                nc.sync.dma_start(out_v[u][:, :, cols], res[:])
+            mx(acc[:], z_q[u // 2][:, m], z_s[u // 2][:, m], z2_q[:], z2_s[:])
+            nc.scalar.activation(wins[u][:, :N], acc[:], ACT.Copy, scale=0.0625)
+            width = N // pieces
+            for c in range(pieces):
+                entries = nb_l[:, width // 16 * c : width // 16 * (c + 1)]
+                nc.vector.tensor_copy(got[u][:, width * c : width * (c + 1)], wins[u][:].indirect(entries))
+
+        def finish(u, res, pieces):
+            width = N // pieces
+            for c in range(pieces):
+                cols = slice(width * c, width * (c + 1))
+                nc.vector.tensor_tensor(res[:, cols], wins[u][:, cols], got[u][:, cols], ALU.max)
+                nc.sync.dma_start(out_v[u][:, :, cols], res[:, cols])
+
+        fetch(0, 1)
+        fetch(1, 1)
+        finish(0, wins[1][:, N:], 1)
+        finish(1, wins[0][:, N:], 1)
+        for u in (2, 3):
+            fetch(u, 2)
+            finish(u, wins[u][:, N:], 2)

@@ -18,10 +18,15 @@ ALU = mybir.AluOpType
 
 P = 128
 PACK = 4
+BANK = 512
 HALF = 256
+LIST_COLS = HALF // 16
+PLACE_RUN = 8
+ROW_RUN = 4
+CV_SCALE = 0.0625
 EARLY = 384
 SHARE = 384
-LIST_COLS = HALF // 16
+STAGE = 896
 
 
 def tile_picked_mommax_none_p_kernel(
@@ -36,7 +41,7 @@ def tile_picked_mommax_none_p_kernel(
             return keep.tile(shape, dtype, name=name, tag=tag or name, align_bytes=64)
 
         def bank(tag, name):
-            return psum.tile([P, 512], F32, name=name, tag=tag)
+            return psum.tile([P, BANK], F32, name=name, tag=tag)
 
         offs_l = sb("offs_l", [P, S // 16], U16)
         two_l = sb("two_l", [P, S // 16], U16)
@@ -50,9 +55,6 @@ def tile_picked_mommax_none_p_kernel(
 
         nc.gpsimd.memset(xs[:].bitcast(I32), 0)
         nc.gpsimd.memset(rows[:], 0.0)
-        wins = [sb("win%d" % t, [P, 2 * H], F32) for t in range(PACK)]
-        for win in wins:
-            nc.vector.memset(win[:, H:], 0.0)
         wa_late = sb("wa_late", [P, PACK, H - EARLY], F32)[:]
         wb_raw = [sb("wb_raw%d" % h, [P, PACK, HALF], F32)[:] for h in range(2)]
 
@@ -63,10 +65,10 @@ def tile_picked_mommax_none_p_kernel(
         wa_v = wa.rearrange("(p j) c -> p j c", j=PACK)
         nc.sync.dma_start(wa_early[:], wa_v[:, :, 0:EARLY])
         nc.sync.dma_start(xw[:], x_words[0].rearrange("p c r -> p (c r)").bitcast(I32))
-        for r, g in enumerate((gt, gi)):
+        for r, weight in enumerate((gt, gi)):
             nc.sync.dma_start(
-                rows[PACK * r : PACK * (r + 1), :].rearrange("t (q e) -> t q e", e=8),
-                g.rearrange("(q t e) o -> t q (e o)", t=PACK, e=8),
+                rows[PACK * r : PACK * (r + 1), :].rearrange("t (q e) -> t q e", e=PLACE_RUN),
+                weight.rearrange("(q t e) o -> t q (e o)", t=PACK, e=PLACE_RUN),
             )
         make_identity(nc, ident[:])
         nc.sync.dma_start(wa_late, wa_v[:, :, EARLY:H])
@@ -76,28 +78,29 @@ def tile_picked_mommax_none_p_kernel(
             nc.sync.dma_start(wb_raw[h], wb_v[:, :, HALF * h : HALF * (h + 1)])
         nc.sync.dma_start(nb_l[:], nb)
 
-        def gather_scales(name, lst):
+        def gather_scales(name, entries):
             picked = sb(name + "_picked", [P, S], U8)
             dealt = sb(name + "_dealt", [P, S], U8)
-            nc.vector.tensor_copy(picked[:], xs[:].indirect(lst[:]))
+            nc.vector.tensor_copy(picked[:], xs[:].indirect(entries[:]))
             nc.vector.tensor_copy(
-                dealt[:].bitcast(I32).rearrange("p (t q w) -> p t q w", t=PACK, w=2),
-                picked[:].bitcast(I32).rearrange("p (q t w) -> p t q w", t=PACK, w=2),
+                dealt[:].bitcast(I32).rearrange("p (t q w) -> p t q w", t=PACK, w=PLACE_RUN // 4),
+                picked[:].bitcast(I32).rearrange("p (q t w) -> p t q w", t=PACK, w=PLACE_RUN // 4),
             )
             return dealt
 
-        def gather_words(name, lst, tag):
+        def gather_words(name, entries, tag):
             dealt = sb(name, [P, S], U32, tag)
             nc.vector.tensor_copy(
-                dealt[:].rearrange("p (t q e) -> p q t e", t=PACK, e=8), xw[:].bitcast(U32).indirect(lst[:])
+                dealt[:].rearrange("p (t q e) -> p q t e", t=PACK, e=PLACE_RUN),
+                xw[:].bitcast(U32).indirect(entries[:]),
             )
             return dealt
 
         def weave(dst):
-            return dst.rearrange("p (c i) t -> p c t i", i=4)
+            return dst.rearrange("p (c i) t -> p c t i", i=ROW_RUN)
 
         def planes(src):
-            return src.rearrange("p t (c i) -> p c t i", i=4)
+            return src.rearrange("p t (c i) -> p c t i", i=ROW_RUN)
 
         def quantize(codes, scales, woven):
             nc.vector.quantize_mx(out=codes.bitcast(FP8X4), scales=scales, in_=woven.rearrange("p c t -> p (c t)"))
@@ -113,17 +116,17 @@ def tile_picked_mommax_none_p_kernel(
 
         wa_q = sb("wa_q", [P, H], U32)
         wa_s = sb("wa_s", [P, H], U8)
-        woven = sb("wa_bf0", [P, EARLY, PACK], BF16)
-        nc.scalar.copy(weave(woven[:]), planes(wa_early[:]))
+        wa_early_bf = sb("wa_bf0", [P, EARLY, PACK], BF16)
+        nc.scalar.copy(weave(wa_early_bf[:]), planes(wa_early[:]))
         for cols in (slice(0, HALF), slice(HALF, EARLY)):
-            quantize(wa_q[:, cols], wa_s[:, cols], woven[:, cols, :])
+            quantize(wa_q[:, cols], wa_s[:, cols], wa_early_bf[:, cols, :])
 
         xa_w = gather_words("xa_w", offs_l, None)
         a_fetched = sb("a_fetched", [P, PACK * H], F32)
-        wb_bf = a_fetched[:, 3 * HALF : 7 * HALF].bitcast(BF16).rearrange("p (c t) -> p c t", t=PACK)
-        woven = wb_bf[:, 0 : H - EARLY, :]
-        nc.scalar.copy(weave(woven), planes(wa_late))
-        quantize(wa_q[:, EARLY:H], wa_s[:, EARLY:H], woven)
+        wb_bf = a_fetched[:, STAGE : STAGE + N * PACK // 2].bitcast(BF16).rearrange("p (c t) -> p c t", t=PACK)
+        wa_late_bf = wb_bf[:, 0 : H - EARLY, :]
+        nc.scalar.copy(weave(wa_late_bf), planes(wa_late))
+        quantize(wa_q[:, EARLY:H], wa_s[:, EARLY:H], wa_late_bf)
         xb_w = gather_words("xb_w", two_l, "wa_late")
 
         turned = bank("b3", "turned")
@@ -148,9 +151,14 @@ def tile_picked_mommax_none_p_kernel(
             m = slice(P * t, P * (t + 1))
             acc = bank("a%d" % t, "acc_a%d" % t)
             mx(acc[:], xa_w[:, m], xa_s[:, m], wa_q[:], wa_s[:])
-            nc.scalar.activation(wins[t][:, :H], acc[:], ACT.Copy, scale=gt_abs[:, t : t + 1])
-            nc.sync.dma_start(a_all[:, H * t : H * (t + 1)], wins[t][:, :H])
-            nc.vector.tensor_copy(a_fetched[:, H * t : H * (t + 1)], wins[t][:].indirect(fa_l[:]))
+            a_win = sb("a_win%d" % t, [P, H], F32)
+            nc.scalar.activation(a_win[:], acc[:], ACT.Copy, scale=gt_abs[:, t : t + 1])
+            nc.sync.dma_start(a_all[:, H * t : H * (t + 1)], a_win[:])
+            for h in range(2):
+                nc.vector.tensor_copy(
+                    a_fetched[:, H * t + HALF * h : H * t + HALF * (h + 1)],
+                    a_win[:].indirect(fa_l[:, LIST_COLS * h : LIST_COLS * (h + 1)]),
+                )
 
         z2_planes = sb("z2_planes", [P, PACK, N], BF16)
         for t in range(PACK):
@@ -163,14 +171,14 @@ def tile_picked_mommax_none_p_kernel(
         z_s = [sb("z_s%d" % h, [P, 2 * P], U8) for h in range(2)]
 
         def pool_z(h, tag):
-            woven = sb("z_bf%d" % h, [P, 2 * P, PACK], BF16, tag)
+            z_bf = sb("z_bf%d" % h, [P, 2 * P, PACK], BF16, tag)
             for c in range(2):
                 a_part, fetched_part = (
-                    src[:].rearrange("p (t v u i) -> p u v t i", t=PACK, u=PACK, i=2)[:, 2 * h + c] for src in (a_all, a_fetched)
+                    src[:].rearrange("p (t v u i) -> p u v t i", t=PACK, u=PACK, i=ROW_RUN)[:, 2 * h + c]
+                    for src in (a_all, a_fetched)
                 )
-                dst = woven[:, P * c : P * (c + 1), :].rearrange("p (v i) t -> p v t i", i=2)
-                nc.vector.tensor_tensor(dst, a_part, fetched_part, ALU.max)
-            quantize(z_q[h][:], z_s[h][:], woven[:])
+                nc.vector.tensor_tensor(weave(z_bf[:, P * c : P * (c + 1), :]), a_part, fetched_part, ALU.max)
+            quantize(z_q[h][:], z_s[h][:], z_bf[:])
 
         z2_q = sb("z2_q", [P, N], U32)
         z2_s = sb("z2_s", [P, N], U8)
@@ -182,30 +190,34 @@ def tile_picked_mommax_none_p_kernel(
         quantize(z2_q[:], z2_s[:], z2_bf[:])
         pool_z(1, "z2_bf")
 
-        out_v = out.rearrange("(v u i) n -> u v i n", u=PACK, i=2)
-        got = [sb("cv_fetched%d" % u, [P, N], F32, "z2_bf" if u == 1 else None) for u in range(PACK)]
+        out_v = out.rearrange("(v u i) n -> u v i n", u=PACK, i=ROW_RUN)
+        cv_fetched = [sb("cv_fetched%d" % h, [P, 2 * N], F32, tag) for h, tag in enumerate(("z2_bf", None))]
 
-        def fetch(u, pieces):
+        def fetch(u):
             acc = bank("a%d" % u, "acc_cv%d" % u)
             m = slice(P * (u % 2), P * (u % 2 + 1))
             mx(acc[:], z_q[u // 2][:, m], z_s[u // 2][:, m], z2_q[:], z2_s[:])
-            nc.scalar.activation(wins[u][:, :N], acc[:], ACT.Copy, scale=0.0625)
-            width = N // pieces
-            for c in range(pieces):
-                entries = nb_l[:, width // 16 * c : width // 16 * (c + 1)]
-                nc.vector.tensor_copy(got[u][:, width * c : width * (c + 1)], wins[u][:].indirect(entries))
+            cv_win = sb("cv_win%d" % u, [P, N], F32)
+            nc.scalar.activation(cv_win[:], acc[:], ACT.Copy, scale=CV_SCALE)
+            got = cv_fetched[u // 2][:, N * (u % 2) : N * (u % 2 + 1)]
+            for h in range(2):
+                nc.vector.tensor_copy(
+                    got[:, HALF * h : HALF * (h + 1)], cv_win[:].indirect(nb_l[:, LIST_COLS * h : LIST_COLS * (h + 1)])
+                )
+            return acc, cv_win, got
 
-        def finish(u, res, pieces):
-            width = N // pieces
-            for c in range(pieces):
-                cols = slice(width * c, width * (c + 1))
-                nc.vector.tensor_tensor(res[:, cols], wins[u][:, cols], got[u][:, cols], ALU.max)
-                nc.sync.dma_start(out_v[u][:, :, cols], res[:, cols])
-
-        fetch(0, 1)
-        fetch(1, 1)
-        finish(0, wins[1][:, N:], 1)
-        finish(1, wins[0][:, N:], 1)
-        for u in (2, 3):
-            fetch(u, 2)
-            finish(u, wins[u][:, N:], 2)
+        first_win, first_got = fetch(0)[1:]
+        excess = sb("excess", [P, N], F32)
+        gain = sb("gain", [P, N], F32)
+        first_res = sb("res0", [P, N], F32)
+        nc.gpsimd.tensor_tensor(excess[:], first_got, first_win[:], ALU.subtract)
+        for u in range(1, PACK):
+            acc, got = fetch(u)[::2]
+            for h in range(2):
+                cols = slice(HALF * h, HALF * (h + 1))
+                res = sb("res%d_%d" % (u, h), [P, HALF], F32)
+                nc.vector.scalar_tensor_tensor(res[:], acc[:, cols], CV_SCALE, got[:, cols], ALU.mult, ALU.max)
+                nc.sync.dma_start(out_v[u][:, :, cols], res[:])
+        nc.scalar.activation(gain[:], excess[:], ACT.Relu)
+        nc.gpsimd.tensor_tensor(first_res[:], first_win[:], gain[:], ALU.add)
+        nc.scalar.dma_start(out_v[0], first_res[:])

from contextlib import ExitStack

import concourse.mybir as mybir
from concourse.masks import make_identity

K, T, S, N, H = 512, 2048, 512, 512, 512
FLOPS = 2 * K * S * H + 2 * K * S * N + 2 * S * H * N

F32 = mybir.dt.float32
BF16 = mybir.dt.bfloat16
I32 = mybir.dt.int32
U32 = mybir.dt.uint32
U16 = mybir.dt.uint16
U8 = mybir.dt.uint8
FP8X4 = mybir.dt.float8_e4m3fn_x4
ACT = mybir.ActivationFunctionType
ALU = mybir.AluOpType

P = 128
PACK = 4
BANK = 512
HALF = 256
LIST_COLS = HALF // 16
PLACE_RUN = 8
ROW_RUN = 4
CV_SCALE = 0.0625
EARLY = 384
SHARE = 384
STAGE = 896


def tile_picked_mommax_none_p_kernel(
    tc, x_words, x_scales, wa, wb, gt, gi, offs, two, fa, nb, out
):
    nc = tc.nc
    with ExitStack() as ctx:
        keep = ctx.enter_context(tc.tile_pool(name="keep", bufs=1))
        psum = ctx.enter_context(tc.psum_pool(name="psum", bufs=1))

        def sb(name, shape, dtype, tag=None):
            return keep.tile(shape, dtype, name=name, tag=tag or name, align_bytes=64)

        def bank(tag, name):
            return psum.tile([P, BANK], F32, name=name, tag=tag)

        offs_l = sb("offs_l", [P, S // 16], U16)
        two_l = sb("two_l", [P, S // 16], U16)
        fa_l = sb("fa_l", [P, H // 16], U16)
        nb_l = sb("nb_l", [P, N // 16], U16)
        xs = sb("xs", [P, T], U8)
        xw = sb("xw", [P, T], I32)
        wa_early = sb("wa_early", [P, PACK, EARLY], F32)
        rows = sb("rows", [P, P], F32)
        ident = sb("ident", [P, P], F32)

        nc.gpsimd.memset(xs[:].bitcast(I32), 0)
        nc.gpsimd.memset(rows[:], 0.0)
        wa_late = sb("wa_late", [P, PACK, H - EARLY], F32)[:]
        wb_raw = [sb("wb_raw%d" % h, [P, PACK, HALF], F32)[:] for h in range(2)]

        nc.sync.dma_start(offs_l[:], offs)
        nc.sync.dma_start(two_l[:], two)
        for q in range(4):
            nc.sync.dma_start(xs[32 * q : 32 * q + 4, :].bitcast(I32), x_scales[0, 4 * q : 4 * q + 4, :].bitcast(I32))
        wa_v = wa.rearrange("(p j) c -> p j c", j=PACK)
        nc.sync.dma_start(wa_early[:], wa_v[:, :, 0:EARLY])
        nc.sync.dma_start(xw[:], x_words[0].rearrange("p c r -> p (c r)").bitcast(I32))
        for r, weight in enumerate((gt, gi)):
            nc.sync.dma_start(
                rows[PACK * r : PACK * (r + 1), :].rearrange("t (q e) -> t q e", e=PLACE_RUN),
                weight.rearrange("(q t e) o -> t q (e o)", t=PACK, e=PLACE_RUN),
            )
        make_identity(nc, ident[:])
        nc.sync.dma_start(wa_late, wa_v[:, :, EARLY:H])
        nc.sync.dma_start(fa_l[:], fa)
        wb_v = wb.rearrange("(p j) c -> p j c", j=PACK)
        for h in range(2):
            nc.sync.dma_start(wb_raw[h], wb_v[:, :, HALF * h : HALF * (h + 1)])
        nc.sync.dma_start(nb_l[:], nb)

        def gather_scales(name, entries):
            picked = sb(name + "_picked", [P, S], U8)
            dealt = sb(name + "_dealt", [P, S], U8)
            nc.vector.tensor_copy(picked[:], xs[:].indirect(entries[:]))
            nc.vector.tensor_copy(
                dealt[:].bitcast(I32).rearrange("p (t q w) -> p t q w", t=PACK, w=PLACE_RUN // 4),
                picked[:].bitcast(I32).rearrange("p (q t w) -> p t q w", t=PACK, w=PLACE_RUN // 4),
            )
            return dealt

        def gather_words(name, entries, tag):
            dealt = sb(name, [P, S], U32, tag)
            nc.vector.tensor_copy(
                dealt[:].rearrange("p (t q e) -> p q t e", t=PACK, e=PLACE_RUN),
                xw[:].bitcast(U32).indirect(entries[:]),
            )
            return dealt

        def weave(dst):
            return dst.rearrange("p (c i) t -> p c t i", i=ROW_RUN)

        def planes(src):
            return src.rearrange("p t (c i) -> p c t i", i=ROW_RUN)

        def quantize(codes, scales, woven):
            nc.vector.quantize_mx(out=codes.bitcast(FP8X4), scales=scales, in_=woven.rearrange("p c t -> p (c t)"))

        def mx(acc, lhs, lhs_s, rhs, rhs_s):
            nc.tensor.matmul_mx(
                out=acc, lhsT=lhs.bitcast(FP8X4), lhsT_scale=lhs_s, rhs=rhs.bitcast(FP8X4), rhs_scale=rhs_s,
                start=True, stop=True,
            )

        xa_s = gather_scales("xa_s", offs_l)
        xb_s = gather_scales("xb_s", two_l)

        wa_q = sb("wa_q", [P, H], U32)
        wa_s = sb("wa_s", [P, H], U8)
        wa_early_bf = sb("wa_bf0", [P, EARLY, PACK], BF16)
        nc.scalar.copy(weave(wa_early_bf[:]), planes(wa_early[:]))
        for cols in (slice(0, HALF), slice(HALF, EARLY)):
            quantize(wa_q[:, cols], wa_s[:, cols], wa_early_bf[:, cols, :])

        xa_w = gather_words("xa_w", offs_l, None)
        a_fetched = sb("a_fetched", [P, PACK * H], F32)
        wb_bf = a_fetched[:, STAGE : STAGE + N * PACK // 2].bitcast(BF16).rearrange("p (c t) -> p c t", t=PACK)
        wa_late_bf = wb_bf[:, 0 : H - EARLY, :]
        nc.scalar.copy(weave(wa_late_bf), planes(wa_late))
        quantize(wa_q[:, EARLY:H], wa_s[:, EARLY:H], wa_late_bf)
        xb_w = gather_words("xb_w", two_l, "wa_late")

        turned = bank("b3", "turned")
        nc.tensor.transpose(turned[:, :P], rows[:], ident[:])
        gt_abs = sb("gt_abs", [P, PACK], F32)
        gt_sign = sb("gt_sign", [P, PACK], F32)
        gi_signed = sb("gi_signed", [P, PACK], F32)
        nc.scalar.activation(gt_abs[:], turned[:, 0:PACK], ACT.Abs)
        nc.scalar.activation(gt_sign[:], turned[:, 0:PACK], ACT.Sign)
        nc.vector.tensor_tensor(gi_signed[:], turned[:, PACK : 2 * PACK], gt_sign[:], ALU.mult)

        wb_q = sb("wb_q", [P, N], U32)
        wb_s = sb("wb_s", [P, N], U8)
        for h in range(2):
            nc.gpsimd.tensor_scalar(
                wb_bf[:, HALF * h : HALF * (h + 1), :], wb_raw[h].rearrange("p t c -> p c t"), 1.0, 0.0, ALU.mult, ALU.add
            )
        quantize(wb_q[:], wb_s[:], wb_bf)

        a_all = sb("a_all", [P, PACK * H], F32)
        for t in range(PACK):
            m = slice(P * t, P * (t + 1))
            acc = bank("a%d" % t, "acc_a%d" % t)
            mx(acc[:], xa_w[:, m], xa_s[:, m], wa_q[:], wa_s[:])
            a_win = sb("a_win%d" % t, [P, H], F32)
            nc.scalar.activation(a_win[:], acc[:], ACT.Copy, scale=gt_abs[:, t : t + 1])
            nc.sync.dma_start(a_all[:, H * t : H * (t + 1)], a_win[:])
            for h in range(2):
                nc.vector.tensor_copy(
                    a_fetched[:, H * t + HALF * h : H * t + HALF * (h + 1)],
                    a_win[:].indirect(fa_l[:, LIST_COLS * h : LIST_COLS * (h + 1)]),
                )

        z2_planes = sb("z2_planes", [P, PACK, N], BF16)
        for t in range(PACK):
            m = slice(P * t, P * (t + 1))
            acc = bank("b%d" % t, "acc_b%d" % t)
            mx(acc[:], xb_w[:, m], xb_s[:, m], wb_q[:], wb_s[:])
            nc.scalar.activation(z2_planes[:, t, :], acc[:], ACT.Copy, scale=gi_signed[:, t : t + 1])

        z_q = [sb("z_q%d" % h, [P, 2 * P], U32) for h in range(2)]
        z_s = [sb("z_s%d" % h, [P, 2 * P], U8) for h in range(2)]

        def pool_z(h, tag):
            z_bf = sb("z_bf%d" % h, [P, 2 * P, PACK], BF16, tag)
            for c in range(2):
                a_part, fetched_part = (
                    src[:].rearrange("p (t v u i) -> p u v t i", t=PACK, u=PACK, i=ROW_RUN)[:, 2 * h + c]
                    for src in (a_all, a_fetched)
                )
                nc.vector.tensor_tensor(weave(z_bf[:, P * c : P * (c + 1), :]), a_part, fetched_part, ALU.max)
            quantize(z_q[h][:], z_s[h][:], z_bf[:])

        z2_q = sb("z2_q", [P, N], U32)
        z2_s = sb("z2_s", [P, N], U8)
        z2_bf = sb("z2_bf", [P, N, PACK], BF16)

        pool_z(0, None)
        nc.scalar.copy(weave(z2_bf[:, 0:SHARE, :]), planes(z2_planes[:, :, 0:SHARE]))
        nc.vector.tensor_copy(weave(z2_bf[:, SHARE:N, :]), planes(z2_planes[:, :, SHARE:N]))
        quantize(z2_q[:], z2_s[:], z2_bf[:])
        pool_z(1, "z2_bf")

        out_v = out.rearrange("(v u i) n -> u v i n", u=PACK, i=ROW_RUN)
        cv_fetched = [sb("cv_fetched%d" % h, [P, 2 * N], F32, tag) for h, tag in enumerate(("z2_bf", None))]

        def fetch(u):
            acc = bank("a%d" % u, "acc_cv%d" % u)
            m = slice(P * (u % 2), P * (u % 2 + 1))
            mx(acc[:], z_q[u // 2][:, m], z_s[u // 2][:, m], z2_q[:], z2_s[:])
            cv_win = sb("cv_win%d" % u, [P, N], F32)
            nc.scalar.activation(cv_win[:], acc[:], ACT.Copy, scale=CV_SCALE)
            got = cv_fetched[u // 2][:, N * (u % 2) : N * (u % 2 + 1)]
            for h in range(2):
                nc.vector.tensor_copy(
                    got[:, HALF * h : HALF * (h + 1)], cv_win[:].indirect(nb_l[:, LIST_COLS * h : LIST_COLS * (h + 1)])
                )
            return acc, cv_win, got

        first_win, first_got = fetch(0)[1:]
        excess = sb("excess", [P, N], F32)
        gain = sb("gain", [P, N], F32)
        first_res = sb("res0", [P, N], F32)
        nc.gpsimd.tensor_tensor(excess[:], first_got, first_win[:], ALU.subtract)
        for u in range(1, PACK):
            acc, got = fetch(u)[::2]
            for h in range(2):
                cols = slice(HALF * h, HALF * (h + 1))
                res = sb("res%d_%d" % (u, h), [P, HALF], F32)
                nc.vector.scalar_tensor_tensor(res[:], acc[:, cols], CV_SCALE, got[:, cols], ALU.mult, ALU.max)
                nc.sync.dma_start(out_v[u][:, :, cols], res[:])
        nc.scalar.activation(gain[:], excess[:], ACT.Relu)
        nc.gpsimd.tensor_tensor(first_res[:], first_win[:], gain[:], ALU.add)
        nc.scalar.dma_start(out_v[0], first_res[:])
